import numpy as np
import ml_dtypes


def mxq(x, axis, fmt="e4m3"):
    dtype, down = {"e4m3": (ml_dtypes.float8_e4m3fn, 7), "e5m2": (ml_dtypes.float8_e5m2, 14)}[fmt]
    v = np.moveaxis(np.asarray(x, np.float32).astype(ml_dtypes.bfloat16).astype(np.float64), axis, -1)
    blocks = v.reshape(v.shape[:-1] + (-1, 32))
    amax = np.abs(blocks).max(-1, keepdims=True)
    byte = np.maximum(np.where(amax > 0, np.frexp(amax)[1] - 1 + 127, 0) - down, 1)
    scale = np.exp2(byte - 127.0)
    codes = (blocks / scale).astype(np.float32).astype(dtype).astype(np.float64)
    return np.moveaxis((codes * scale).reshape(v.shape), -1, axis)


WIDE = False


def mx_kscale(k):
    if not WIDE:
        return np.ones(k)
    levels = np.array([30, -30])
    if k % 512:
        return np.exp2(np.random.permutation(np.resize(levels, k // 32))).repeat(32)
    a = np.empty((k // 512, 16))
    for p in range(k // 512):
        a[p, :8] = np.random.permutation(np.resize(levels, 8))
        for g in range(8):
            far = levels[np.abs(levels - a[p, g]) >= 10]
            a[p, g + 8] = far[np.random.randint(len(far))]
    return np.exp2(a.ravel()).repeat(32)


BF16 = ml_dtypes.bfloat16


def bf(x):
    return np.asarray(x, np.float32).astype(BF16)


def f64(x):
    return np.asarray(x).astype(np.float64)


E2M1 = np.array([0.0, 0.5, 1.0, 1.5, 2.0, 3.0, 4.0, 6.0, -0.0, -0.5, -1.0, -1.5, -2.0, -3.0, -4.0, -6.0])


def pack_weight(w, fmt):
    k, n = w.shape
    w = f64(bf(w)).reshape(k // 32, 32, n)
    amax = np.abs(w).max(1)
    if fmt == "e4m3":
        byte = np.frexp(amax)[1] - 1 + 127 - 7
    else:
        mant, ex = np.frexp(amax / 6.0)
        byte = np.where(mant > 0.5, ex, ex - 1) + 127
    byte = np.clip(np.where(amax > 0, byte, 1), 1, 254)
    scaled = (w * np.exp2(127.0 - byte)[:, None, :]).reshape(k, n).astype(np.float32)
    by_word = np.ascontiguousarray(scaled.reshape(k // 512, 128, 4, n).transpose(0, 1, 3, 2))
    if fmt == "e4m3":
        words = by_word.astype(ml_dtypes.float8_e4m3fn).view(np.uint8)
    else:
        c = by_word.astype(ml_dtypes.float4_e2m1fn).view(np.uint8) & 0xF
        words = c[..., 0::2] | (c[..., 1::2] << 4)
    return np.ascontiguousarray(words), np.ascontiguousarray(byte.astype(np.uint8).reshape(k // 512, 16, n))


def unpack_weight(words, scales, fmt):
    g, p, n, _ = words.shape
    if fmt == "e4m3":
        vals = np.ascontiguousarray(words).view(ml_dtypes.float8_e4m3fn).astype(np.float64)
    else:
        nib = np.empty((g, p, n, 4), np.uint8)
        nib[..., 0::2] = words & 0xF
        nib[..., 1::2] = words >> 4
        vals = E2M1[nib]
    vals = vals * np.repeat(np.exp2(scales.astype(np.float64) - 127.0), 8, axis=1)[..., None]
    return vals.transpose(0, 1, 3, 2).reshape(g * 512, n)
def pack4(w):
    words, scales = pack_weight(w, "e2m1")
    return words.reshape(words.shape[0], 128, -1), scales


def unpack4(words, scales):
    return unpack_weight(words.reshape(words.shape[0], 128, -1, 2), scales, "e2m1")


M, K, H, N = 1024, 2048, 1024, 2048


def setup_inputs():
    s = mx_kscale(K)
    t = mx_kscale(H)
    h = np.arange(H)
    order, phase = 1 + h // 2, (h % 2) * np.pi / 2
    az_fit = np.random.uniform(0, 2 * np.pi, K)
    az_new = np.random.uniform(0, 2 * np.pi, N)
    fit = np.sqrt(2 / K) * np.cos(az_fit[:, None] * order - phase)
    basis = np.sqrt(2 / H) * np.cos(order[:, None] * az_new - phase[:, None])
    fit_words, fit_scales = pack4(fit / s[:, None])
    return {"vel": bf(np.random.standard_normal((M, K)) * s),
            "fit_words": fit_words,
            "fit_scales": fit_scales,
            "damp": bf(np.random.uniform(0.5, 1.0, H) * t),
            "basis": bf(basis / t[:, None]),
            "obs": bf(np.random.standard_normal((M, N)))}


def reference(vel, fit_words, fit_scales, damp, basis, obs):
    c = mxq(f64(vel), 1, "e4m3") @ unpack4(fit_words, fit_scales)
    c = c * f64(damp)
    v = mxq(c, 1, "e5m2") @ mxq(f64(basis), 0, "e4m3")
    r = f64(obs) - v
    return r * np.exp(-0.5 * np.square(r))

@@ -1,0 +1,275 @@
+from contextlib import ExitStack
+
+import concourse.mybir as mybir
+from concourse.masks import make_identity
+
+M, K, H, N = 1024, 2048, 1024, 2048
+FLOPS = 2 * M * K * H + 2 * M * H * N
+
+F32 = mybir.dt.float32
+BF16 = mybir.dt.bfloat16
+U32 = mybir.dt.uint32
+I32 = mybir.dt.int32
+U8 = mybir.dt.uint8
+E4M3X4 = mybir.dt.float8_e4m3fn_x4
+E5M2X4 = mybir.dt.float8_e5m2_x4
+E2M1X4 = mybir.dt.float4_e2m1fn_x4
+ALU = mybir.AluOpType
+ACT = mybir.ActivationFunctionType
+
+P = 128
+BANK = 512
+PASS = 512
+K_PASSES = K // PASS
+H_PASSES = H // PASS
+M_TILES = M // P
+N_BLOCKS = N // BANK
+HALF = N // 2
+ON_SCALAR = (0, 2, 3, 5, 7)
+WARM = 0
+FINE = 512
+LAG = 2
+LOADS = "v0 s0 b0 b1 v1 f0 f1 b2 v2 b3 o0 b4 v3 b5 o1 b6 b7".split()
+UNITS = {-3: ((0,), (1,)), -2: ((), (2,)), -1: ((), (3,)), 0: ((4,), (5,)), 1: ((6,), (7,))}
+GP = 0
+
+
+def tile_vad_harmonic_residuals_s9_kernel(tc, vel, fit_words, fit_scales, damp, basis, obs, out):
+    nc = tc.nc
+    with ExitStack() as ctx:
+        keep = ctx.enter_context(tc.tile_pool(name="keep", bufs=1))
+        work = ctx.enter_context(tc.tile_pool(name="work", bufs=2))
+        psum = ctx.enter_context(tc.psum_pool(name="psum", bufs=1))
+        ctx.enter_context(tc.manual_schedule(engines={mybir.EngineType.SP}))
+
+        ident = keep.tile([P, P], F32, name="ident")
+        fit_plane = keep.tile([P, K_PASSES, H], U8, name="fit_plane", align_bytes=64)
+        damp_rows = keep.tile([P, H_PASSES, 4], BF16, name="damp_rows")
+        damp_all = keep.tile([P, H], BF16, name="damp_all", align_bytes=64)
+        t = {}
+
+        def load_vel(i):
+            t["vel", i] = work.tile([P, K], BF16, name="vel_raw", bufs=4)
+            nc.sync.dma_start(out=t["vel", i][:], in_=vel[i * P : (i + 1) * P, :])
+
+        def load_obs(i):
+            t["obs", i] = work.tile([P, N], BF16, name="obs_raw", bufs=3 + LAG)
+            nc.sync.dma_start(out=t["obs", i][:], in_=obs[i * P : (i + 1) * P, :])
+
+        def load_fit(j):
+            t["fit", j] = keep.tile([P, 2, 2 * H], U8, name="fit%d" % j, align_bytes=64)
+            nc.sync.dma_start(
+                out=t["fit", j][:].bitcast(I32),
+                in_=fit_words[2 * j : 2 * j + 2].bitcast(I32).rearrange("g p c -> p g c"),
+            )
+
+        def load_fit_scales():
+            for q in range(4):
+                nc.sync.dma_start(
+                    out=fit_plane[32 * q : 32 * q + 4].bitcast(I32),
+                    in_=fit_scales[:, 4 * q : 4 * q + 4, :].bitcast(I32).rearrange("g r c -> r g c"),
+                )
+
+        def load_small(u):
+            nc.sync.dma_start(out=damp_rows[:], in_=damp.rearrange("(g p j) -> p g j", g=H_PASSES, j=4))
+            load_fit_scales()
+
+        def load_basis(u):
+            b, g = divmod(u, H_PASSES)
+            t["basis", u] = keep.tile([P, 4, BANK], BF16, name="basis_raw%d" % u)
+            rows = basis[g * PASS : (g + 1) * PASS, b * BANK : (b + 1) * BANK]
+            nc.sync.dma_start(out=t["basis", u][:], in_=rows.rearrange("(p j) n -> p j n", j=4))
+
+        def group_basis(u):
+            t["basis_grouped", u] = work.tile([P, BANK, 4], BF16, name="basis_grouped", bufs=3, align_bytes=64)
+            dst = t["basis_grouped", u][:].rearrange("p (c i) j -> p c j i", i=4)
+            src = t["basis", u][:].rearrange("p j (c i) -> p c j i", i=4)
+            if u == 0:
+                nc.scalar.activation(out=dst, in_=src, func=ACT.Copy)
+            elif u in ON_SCALAR:
+                nc.scalar.copy(out=dst, in_=src)
+            else:
+                nc.vector.tensor_copy(out=dst, in_=src)
+
+        def quantise_basis(u):
+            t["basis_codes", u] = keep.tile([P, BANK], U32, name="basis_codes%d" % u, align_bytes=64)
+            t["basis_scales", u] = keep.tile([P, BANK], U8, name="basis_scales%d" % u, align_bytes=64)
+            nc.vector.quantize_mx(
+                out=t["basis_codes", u][:].bitcast(E4M3X4),
+                scales=t["basis_scales", u][:],
+                in_=t["basis_grouped", u][:].rearrange("p n j -> p (n j)"),
+            )
+
+        def spread_damp():
+            bank = psum.tile([P, 4, P], F32, name="bank", bufs=8)
+            words = damp_rows[:].rearrange("p g j -> p (g j)").bitcast(F32)
+            for c in range(4):
+                nc.tensor.transpose(bank[:, c, :], words[:, c : c + 1].to_broadcast([P, P]), ident[:])
+            nc.scalar.copy(out=damp_all[:].bitcast(F32), in_=bank[:].rearrange("p c m -> p (c m)"))
+
+        def turn_vel(i):
+            words = t["vel", i][:].bitcast(F32)
+            for j in range(2):
+                t["vel_bank", i, j] = psum.tile([P, 2, 2, P], F32, name="bank", bufs=8)
+                for g in range(2):
+                    w0 = (2 * j + g) * PASS // 2
+                    for u in range(2):
+                        nc.tensor.transpose(t["vel_bank", i, j][:, g, u, :], words[:, w0 + u : w0 + PASS // 2 : 2], ident[:])
+
+        def group_vel(i, j):
+            if j == 0:
+                t["vel_grouped", i] = work.tile([P, K_PASSES, P, 4], BF16, name="vel_grouped", align_bytes=64)
+            dst = t["vel_grouped", i][:, 2 * j : 2 * j + 2].bitcast(F32)
+            nc.scalar.copy(out=dst, in_=t["vel_bank", i, j][:].rearrange("p g u m -> p g m u"))
+
+        def quantise_vel(i):
+            t["vel_codes", i] = work.tile([P, K_PASSES * P], U32, name="vel_codes", align_bytes=64)
+            t["vel_scales", i] = work.tile([P, K_PASSES * P], U8, name="vel_scales", align_bytes=64)
+            nc.vector.quantize_mx(
+                out=t["vel_codes", i][:].bitcast(E4M3X4),
+                scales=t["vel_scales", i][:],
+                in_=t["vel_grouped", i][:].rearrange("p g m j -> p (g m j)"),
+            )
+
+        def project(i, hh):
+            t["c_bank", i, hh] = psum.tile([P, BANK], F32, name="bank", bufs=8)
+            for g in range(K_PASSES):
+                nc.tensor.matmul_mx(
+                    out=t["c_bank", i, hh][:],
+                    lhsT=t["vel_codes", i][:, g * P : (g + 1) * P].bitcast(E4M3X4),
+                    lhsT_scale=t["vel_scales", i][:, g * P : (g + 1) * P],
+                    rhs=t["fit", g // 2][:, g % 2, 2 * hh * BANK : 2 * (hh + 1) * BANK].bitcast(E2M1X4),
+                    rhs_scale=fit_plane[:, g, hh * BANK : (hh + 1) * BANK],
+                    start=(g == 0),
+                    stop=(g == K_PASSES - 1),
+                )
+
+        def apply_damp(i, hh):
+            if hh == 0:
+                t["c_rows", i] = work.tile([P, H], BF16, name="c_rows")
+            cols = slice(hh * BANK, (hh + 1) * BANK)
+            nc.vector.tensor_tensor(
+                out=t["c_rows", i][:, cols].rearrange("m (u p e) -> m u p e", u=2, e=2),
+                in0=t["c_bank", i, hh][:].rearrange("m (p u e) -> m u p e", u=2, e=2),
+                in1=damp_all[:, cols].rearrange("m (u p e) -> m u p e", u=2, e=2),
+                op=ALU.mult,
+            )
+
+        def turn_c(i):
+            words = t["c_rows", i][:].bitcast(F32)
+            t["c_turned", i] = psum.tile([P, 2, 2, P], F32, name="bank", bufs=8)
+            for g in range(H_PASSES):
+                for u in range(2):
+                    w0 = (2 * g + u) * P
+                    nc.tensor.transpose(t["c_turned", i][:, g, u, :], words[:, w0 : w0 + P], ident[:])
+
+        def group_c(i):
+            t["c_grouped", i] = work.tile([P, H_PASSES, P, 4], BF16, name="c_grouped", align_bytes=64)
+            nc.scalar.copy(out=t["c_grouped", i][:].bitcast(F32), in_=t["c_turned", i][:].rearrange("p g u m -> p g m u"))
+
+        def quantise_c(i):
+            t["c_codes", i] = work.tile([P, H_PASSES * P], U32, name="c_codes", bufs=3 + LAG, align_bytes=64)
+            t["c_scales", i] = work.tile([P, H_PASSES * P], U8, name="c_scales", bufs=3 + LAG, align_bytes=64)
+            nc.vector.quantize_mx(
+                out=t["c_codes", i][:].bitcast(E5M2X4),
+                scales=t["c_scales", i][:],
+                in_=t["c_grouped", i][:].rearrange("p g m j -> p (g m j)"),
+            )
+
+        def evaluate(i, b):
+            t["v_bank", i, b] = psum.tile([P, BANK], F32, name="bank", bufs=8)
+            for g in range(H_PASSES):
+                nc.tensor.matmul_mx(
+                    out=t["v_bank", i, b][:],
+                    lhsT=t["c_codes", i][:, g * P : (g + 1) * P].bitcast(E5M2X4),
+                    lhsT_scale=t["c_scales", i][:, g * P : (g + 1) * P],
+                    rhs=t["basis_codes", H_PASSES * b + g][:].bitcast(E4M3X4),
+                    rhs_scale=t["basis_scales", H_PASSES * b + g][:],
+                    start=(g == 0),
+                    stop=(g == H_PASSES - 1),
+                )
+
+        def subtract(i, b):
+            half, side = divmod(b, 2)
+            if side == 0:
+                t["r", i, half] = work.tile([P, HALF], F32, name="residual", bufs=4)
+            nc.vector.tensor_tensor(
+                out=t["r", i, half][:, side * BANK : (side + 1) * BANK],
+                in0=t["obs", i][:, b * BANK : (b + 1) * BANK],
+                in1=t["v_bank", i, b][:],
+                op=ALU.subtract,
+            )
+
+        def pieces(i, half):
+            if i == M_TILES - 1 and half == 1:
+                return [slice(c, c + FINE) for c in range(0, HALF, FINE)]
+            return [slice(0, HALF)]
+
+        def square(i, half):
+            t["sq", i, half] = work.tile([P, HALF], F32, name="squares", bufs=3)
+            for c in pieces(i, half):
+                nc.scalar.activation(out=t["sq", i, half][:, c], in_=t["r", i, half][:, c], func=ACT.Square)
+
+        def gauss(i, half):
+            t["w", i, half] = work.tile([P, HALF], F32, name="weights", bufs=3)
+            for c in pieces(i, half):
+                nc.scalar.activation(out=t["w", i, half][:, c], in_=t["sq", i, half][:, c], func=ACT.Exp, scale=-0.5)
+
+        def weigh(i, half):
+            res = work.tile([P, HALF], F32, name="result", bufs=4)
+            eng = nc.gpsimd if (GP and half == 1) else nc.vector
+            for c in pieces(i, half):
+                eng.tensor_tensor(out=res[:, c], in0=t["r", i, half][:, c], in1=t["w", i, half][:, c], op=ALU.mult)
+                nc.sync.dma_start(out=out[i * P : (i + 1) * P, half * HALF : (half + 1) * HALF][:, c], in_=res[:, c])
+
+        def when(i, f, *rest):
+            if 0 <= i < M_TILES:
+                f(i, *rest)
+
+        nc.vector.memset(fit_plane[:].bitcast(I32), 0)
+        make_identity(nc, ident[:])
+        if WARM:
+            warm = keep.tile([P, 1], F32, name="warm")
+            nc.scalar.activation(out=warm[:], in_=ident[:, 0:1], func=ACT.Exp)
+        for item in LOADS:
+            dict(v=load_vel, f=load_fit, b=load_basis, o=load_obs, s=load_small)[item[0]](int(item[1]))
+
+        for s in range(-3, M_TILES + LAG + 1):
+            first, second = UNITS.get(s, ((), ()))
+            r = s - LAG
+            if s >= 0:
+                when(s + 4, load_vel)
+                when(s + 2, load_obs)
+            when(s, evaluate, 0)
+            when(s, evaluate, 1)
+            when(s + 2, quantise_vel)
+            when(s + 1, apply_damp, 0)
+            when(s + 1, apply_damp, 1)
+            when(s + 3, turn_vel)
+            when(s + 1, turn_c)
+            when(r - 1, square, 1)
+            when(s - 1, gauss, 0)
+            when(s, subtract, 0)
+            when(s, subtract, 1)
+            when(s + 3, group_vel, 0)
+            when(s + 1, group_c)
+            for u in first:
+                group_basis(u)
+            when(s - 1, weigh, 0)
+            when(r, evaluate, 2)
+            when(r, evaluate, 3)
+            if s == -2:
+                spread_damp()
+            when(s + 2, project, 0)
+            when(s + 2, project, 1)
+            when(r - 1, gauss, 1)
+            when(s + 3, group_vel, 1)
+            when(s + 1, quantise_c)
+            when(r, subtract, 2)
+            when(r, subtract, 3)
+            when(s, square, 0)
+            for u in second:
+                group_basis(u)
+            when(r - 1, weigh, 1)
+            for u in first + second:
+                quantise_basis(u)

@@ -18,20 +18,21 @@ ALU = mybir.AluOpType
 ACT = mybir.ActivationFunctionType
 
 P = 128
+PACK = 4
+PASS = P * PACK
 BANK = 512
-PASS = 512
 K_PASSES = K // PASS
 H_PASSES = H // PASS
-M_TILES = M // P
-N_BLOCKS = N // BANK
+ROW_TILES = M // P
 HALF = N // 2
-ON_SCALAR = (0, 2, 3, 5, 7)
-WARM = 0
-FINE = 512
+PIECES = (N // BANK) * H_PASSES
+
+FIRST_STEP = -3
 LAG = 2
-LOADS = "v0 s0 b0 b1 v1 f0 f1 b2 v2 b3 o0 b4 v3 b5 o1 b6 b7".split()
-UNITS = {-3: ((0,), (1,)), -2: ((), (2,)), -1: ((), (3,)), 0: ((4,), (5,)), 1: ((6,), (7,))}
-GP = 0
+SHARED_FROM = 3
+SHARED_TO = 8
+VEL_SPLIT_FROM = 8
+ACTCOPY = 0
 
 
 def tile_vad_harmonic_residuals_s9_kernel(tc, vel, fit_words, fit_scales, damp, basis, obs, out):
@@ -39,237 +40,262 @@ def tile_vad_harmonic_residuals_s9_kernel(tc, vel, fit_words, fit_scales, damp, 
     with ExitStack() as ctx:
         keep = ctx.enter_context(tc.tile_pool(name="keep", bufs=1))
         work = ctx.enter_context(tc.tile_pool(name="work", bufs=2))
-        psum = ctx.enter_context(tc.psum_pool(name="psum", bufs=1))
-        ctx.enter_context(tc.manual_schedule(engines={mybir.EngineType.SP}))
+        psum = ctx.enter_context(tc.psum_pool(name="psum", bufs=8))
+        ctx.enter_context(tc.manual_schedule())
 
         ident = keep.tile([P, P], F32, name="ident")
         fit_plane = keep.tile([P, K_PASSES, H], U8, name="fit_plane", align_bytes=64)
-        damp_rows = keep.tile([P, H_PASSES, 4], BF16, name="damp_rows")
-        damp_all = keep.tile([P, H], BF16, name="damp_all", align_bytes=64)
-        t = {}
+        damp_rows = keep.tile([P, H_PASSES, PACK], BF16, name="damp_rows")
+        damp_all = keep.tile([P, H], BF16, name="damp_all")
+        tiles = {}
 
         def load_vel(i):
-            t["vel", i] = work.tile([P, K], BF16, name="vel_raw", bufs=4)
-            nc.sync.dma_start(out=t["vel", i][:], in_=vel[i * P : (i + 1) * P, :])
+            tiles["vel", i] = keep.tile([P, K], BF16, name="vel%d" % i)
+            nc.sync.dma_start(out=tiles["vel", i][:], in_=vel[i * P : (i + 1) * P, :])
 
-        def load_obs(i):
-            t["obs", i] = work.tile([P, N], BF16, name="obs_raw", bufs=3 + LAG)
-            nc.sync.dma_start(out=t["obs", i][:], in_=obs[i * P : (i + 1) * P, :])
+        def load_obs(i, half):
+            tiles["obs", i, half] = keep.tile([P, HALF], BF16, name="obs%d_%d" % (i, half))
+            nc.sync.dma_start(out=tiles["obs", i, half][:], in_=obs[i * P : (i + 1) * P, half * HALF : (half + 1) * HALF])
 
-        def load_fit(j):
-            t["fit", j] = keep.tile([P, 2, 2 * H], U8, name="fit%d" % j, align_bytes=64)
-            nc.sync.dma_start(
-                out=t["fit", j][:].bitcast(I32),
-                in_=fit_words[2 * j : 2 * j + 2].bitcast(I32).rearrange("g p c -> p g c"),
-            )
+        def load_basis(piece):
+            b, g = divmod(piece, H_PASSES)
+            tiles["basis", piece] = keep.tile([P, PACK, BANK], BF16, name="basis%d" % piece)
+            rows = basis[g * PASS : (g + 1) * PASS, b * BANK : (b + 1) * BANK]
+            nc.sync.dma_start(out=tiles["basis", piece][:], in_=rows.rearrange("(p t) n -> p t n", t=PACK))
 
-        def load_fit_scales():
+        def load_damp_and_fit():
+            nc.sync.dma_start(out=damp_rows[:], in_=damp.rearrange("(g p t) -> p g t", g=H_PASSES, t=PACK))
             for q in range(4):
                 nc.sync.dma_start(
                     out=fit_plane[32 * q : 32 * q + 4].bitcast(I32),
                     in_=fit_scales[:, 4 * q : 4 * q + 4, :].bitcast(I32).rearrange("g r c -> r g c"),
                 )
-
-        def load_small(u):
-            nc.sync.dma_start(out=damp_rows[:], in_=damp.rearrange("(g p j) -> p g j", g=H_PASSES, j=4))
-            load_fit_scales()
-
-        def load_basis(u):
-            b, g = divmod(u, H_PASSES)
-            t["basis", u] = keep.tile([P, 4, BANK], BF16, name="basis_raw%d" % u)
-            rows = basis[g * PASS : (g + 1) * PASS, b * BANK : (b + 1) * BANK]
-            nc.sync.dma_start(out=t["basis", u][:], in_=rows.rearrange("(p j) n -> p j n", j=4))
-
-        def group_basis(u):
-            t["basis_grouped", u] = work.tile([P, BANK, 4], BF16, name="basis_grouped", bufs=3, align_bytes=64)
-            dst = t["basis_grouped", u][:].rearrange("p (c i) j -> p c j i", i=4)
-            src = t["basis", u][:].rearrange("p j (c i) -> p c j i", i=4)
-            if u == 0:
-                nc.scalar.activation(out=dst, in_=src, func=ACT.Copy)
-            elif u in ON_SCALAR:
-                nc.scalar.copy(out=dst, in_=src)
-            else:
-                nc.vector.tensor_copy(out=dst, in_=src)
-
-        def quantise_basis(u):
-            t["basis_codes", u] = keep.tile([P, BANK], U32, name="basis_codes%d" % u, align_bytes=64)
-            t["basis_scales", u] = keep.tile([P, BANK], U8, name="basis_scales%d" % u, align_bytes=64)
-            nc.vector.quantize_mx(
-                out=t["basis_codes", u][:].bitcast(E4M3X4),
-                scales=t["basis_scales", u][:],
-                in_=t["basis_grouped", u][:].rearrange("p n j -> p (n j)"),
-            )
+            for j in range(K_PASSES // 2):
+                tiles["fit", j] = keep.tile([P, 2, 2 * H], U8, name="fit%d" % j, align_bytes=64)
+                nc.sync.dma_start(
+                    out=tiles["fit", j][:].bitcast(I32),
+                    in_=fit_words[2 * j : 2 * j + 2].bitcast(I32).rearrange("g p c -> p g c"),
+                )
 
         def spread_damp():
-            bank = psum.tile([P, 4, P], F32, name="bank", bufs=8)
-            words = damp_rows[:].rearrange("p g j -> p (g j)").bitcast(F32)
-            for c in range(4):
+            bank = psum.tile([P, H_PASSES * 2, P], F32, name="bank")
+            words = damp_rows[:].rearrange("p g t -> p (g t)").bitcast(F32)
+            for c in range(H_PASSES * 2):
                 nc.tensor.transpose(bank[:, c, :], words[:, c : c + 1].to_broadcast([P, P]), ident[:])
-            nc.scalar.copy(out=damp_all[:].bitcast(F32), in_=bank[:].rearrange("p c m -> p (c m)"))
+            nc.scalar.copy(out=damp_all[:].bitcast(F32), in_=bank[:].rearrange("m c p -> m (c p)"))
+
+        def group_basis(piece, engine, grouped=None):
+            if grouped is None:
+                grouped = work.tile([P, BANK * PACK], BF16, name="basis_grouped", align_bytes=64)[:]
+            tiles["basis_grouped", piece] = grouped
+            if engine is nc.gpsimd:
+                nc.gpsimd.tensor_scalar(
+                    out=grouped.rearrange("p (n t) -> p n t", t=PACK),
+                    in0=tiles["basis", piece][:].rearrange("p t n -> p n t"),
+                    scalar1=1.0,
+                    scalar2=0.0,
+                    op0=ALU.mult,
+                    op1=ALU.add,
+                )
+                return
+            dst = grouped.rearrange("p (c i t) -> p c t i", i=4, t=PACK)
+            src = tiles["basis", piece][:].rearrange("p t (c i) -> p c t i", i=4)
+            if engine is nc.vector:
+                nc.vector.tensor_copy(out=dst, in_=src)
+            elif ACTCOPY and piece == 1:
+                nc.scalar.activation(out=dst, in_=src, func=ACT.Copy)
+            else:
+                nc.scalar.copy(out=dst, in_=src)
+
+        def quantise_basis(piece):
+            tiles["basis_codes", piece] = keep.tile([P, BANK], U32, name="basis_codes%d" % piece, align_bytes=64)
+            tiles["basis_scales", piece] = keep.tile([P, BANK], U8, name="basis_scales%d" % piece, align_bytes=64)
+            nc.vector.quantize_mx(
+                out=tiles["basis_codes", piece][:].bitcast(E4M3X4),
+                scales=tiles["basis_scales", piece][:],
+                in_=tiles["basis_grouped", piece],
+            )
 
         def turn_vel(i):
-            words = t["vel", i][:].bitcast(F32)
-            for j in range(2):
-                t["vel_bank", i, j] = psum.tile([P, 2, 2, P], F32, name="bank", bufs=8)
+            words = tiles["vel", i][:].bitcast(F32)
+            for j in range(K_PASSES // 2):
+                tiles["vel_bank", i, j] = psum.tile([P, 2, 2, P], F32, name="bank")
                 for g in range(2):
                     w0 = (2 * j + g) * PASS // 2
                     for u in range(2):
-                        nc.tensor.transpose(t["vel_bank", i, j][:, g, u, :], words[:, w0 + u : w0 + PASS // 2 : 2], ident[:])
+                        nc.tensor.transpose(tiles["vel_bank", i, j][:, g, u, :], words[:, w0 + u : w0 + PASS // 2 : 2], ident[:])
 
-        def group_vel(i, j):
-            if j == 0:
-                t["vel_grouped", i] = work.tile([P, K_PASSES, P, 4], BF16, name="vel_grouped", align_bytes=64)
-            dst = t["vel_grouped", i][:, 2 * j : 2 * j + 2].bitcast(F32)
-            nc.scalar.copy(out=dst, in_=t["vel_bank", i, j][:].rearrange("p g u m -> p g m u"))
+        def group_vel(i):
+            tiles["vel_grouped", i] = work.tile([P, K_PASSES, P, PACK], BF16, name="vel_grouped", align_bytes=64)
+            for j in range(K_PASSES // 2):
+                copy = nc.vector.tensor_copy if (i >= VEL_SPLIT_FROM and j == 1) else nc.scalar.copy
+                copy(
+                    out=tiles["vel_grouped", i][:, 2 * j : 2 * j + 2].bitcast(F32),
+                    in_=tiles["vel_bank", i, j][:].rearrange("p g u m -> p g m u"),
+                )
 
         def quantise_vel(i):
-            t["vel_codes", i] = work.tile([P, K_PASSES * P], U32, name="vel_codes", align_bytes=64)
-            t["vel_scales", i] = work.tile([P, K_PASSES * P], U8, name="vel_scales", align_bytes=64)
+            tiles["vel_codes", i] = work.tile([P, K_PASSES * P], U32, name="vel_codes", align_bytes=64)
+            tiles["vel_scales", i] = work.tile([P, K_PASSES * P], U8, name="vel_scales", align_bytes=64)
             nc.vector.quantize_mx(
-                out=t["vel_codes", i][:].bitcast(E4M3X4),
-                scales=t["vel_scales", i][:],
-                in_=t["vel_grouped", i][:].rearrange("p g m j -> p (g m j)"),
+                out=tiles["vel_codes", i][:].bitcast(E4M3X4),
+                scales=tiles["vel_scales", i][:],
+                in_=tiles["vel_grouped", i][:].rearrange("p g m t -> p (g m t)"),
             )
 
-        def project(i, hh):
-            t["c_bank", i, hh] = psum.tile([P, BANK], F32, name="bank", bufs=8)
-            for g in range(K_PASSES):
-                nc.tensor.matmul_mx(
-                    out=t["c_bank", i, hh][:],
-                    lhsT=t["vel_codes", i][:, g * P : (g + 1) * P].bitcast(E4M3X4),
-                    lhsT_scale=t["vel_scales", i][:, g * P : (g + 1) * P],
-                    rhs=t["fit", g // 2][:, g % 2, 2 * hh * BANK : 2 * (hh + 1) * BANK].bitcast(E2M1X4),
-                    rhs_scale=fit_plane[:, g, hh * BANK : (hh + 1) * BANK],
-                    start=(g == 0),
-                    stop=(g == K_PASSES - 1),
+        def project(i):
+            for hg in range(H_PASSES):
+                tiles["c_bank", i, hg] = psum.tile([P, BANK], F32, name="bank")
+                for g in range(K_PASSES):
+                    nc.tensor.matmul_mx(
+                        out=tiles["c_bank", i, hg][:],
+                        lhsT=tiles["vel_codes", i][:, g * P : (g + 1) * P].bitcast(E4M3X4),
+                        lhsT_scale=tiles["vel_scales", i][:, g * P : (g + 1) * P],
+                        rhs=tiles["fit", g // 2][:, g % 2, 2 * hg * BANK : 2 * (hg + 1) * BANK].bitcast(E2M1X4),
+                        rhs_scale=fit_plane[:, g, hg * BANK : (hg + 1) * BANK],
+                        start=(g == 0),
+                        stop=(g == K_PASSES - 1),
+                    )
+
+        def apply_damp(i):
+            tiles["c_rows", i] = work.tile([P, H], BF16, name="c_rows")
+            for hg in range(H_PASSES):
+                cols = slice(hg * BANK, (hg + 1) * BANK)
+                nc.vector.tensor_tensor(
+                    out=tiles["c_rows", i][:, cols].rearrange("m (u p e) -> m u p e", u=2, e=2),
+                    in0=tiles["c_bank", i, hg][:].rearrange("m (p u e) -> m u p e", u=2, e=2),
+                    in1=damp_all[:, cols].rearrange("m (u p e) -> m u p e", u=2, e=2),
+                    op=ALU.mult,
                 )
-
-        def apply_damp(i, hh):
-            if hh == 0:
-                t["c_rows", i] = work.tile([P, H], BF16, name="c_rows")
-            cols = slice(hh * BANK, (hh + 1) * BANK)
-            nc.vector.tensor_tensor(
-                out=t["c_rows", i][:, cols].rearrange("m (u p e) -> m u p e", u=2, e=2),
-                in0=t["c_bank", i, hh][:].rearrange("m (p u e) -> m u p e", u=2, e=2),
-                in1=damp_all[:, cols].rearrange("m (u p e) -> m u p e", u=2, e=2),
-                op=ALU.mult,
-            )
 
         def turn_c(i):
-            words = t["c_rows", i][:].bitcast(F32)
-            t["c_turned", i] = psum.tile([P, 2, 2, P], F32, name="bank", bufs=8)
-            for g in range(H_PASSES):
+            words = tiles["c_rows", i][:].bitcast(F32)
+            tiles["c_turned", i] = psum.tile([P, H_PASSES, 2, P], F32, name="bank")
+            for hg in range(H_PASSES):
                 for u in range(2):
-                    w0 = (2 * g + u) * P
-                    nc.tensor.transpose(t["c_turned", i][:, g, u, :], words[:, w0 : w0 + P], ident[:])
+                    w0 = (2 * hg + u) * P
+                    nc.tensor.transpose(tiles["c_turned", i][:, hg, u, :], words[:, w0 : w0 + P], ident[:])
 
         def group_c(i):
-            t["c_grouped", i] = work.tile([P, H_PASSES, P, 4], BF16, name="c_grouped", align_bytes=64)
-            nc.scalar.copy(out=t["c_grouped", i][:].bitcast(F32), in_=t["c_turned", i][:].rearrange("p g u m -> p g m u"))
+            tiles["c_grouped", i] = work.tile([P, 2 * H], BF16, name="c_grouped", bufs=3, align_bytes=64)
+            nc.scalar.copy(
+                out=tiles["c_grouped", i][:, :H].bitcast(F32).rearrange("p (g m u) -> p g m u", g=H_PASSES, u=2),
+                in_=tiles["c_turned", i][:].rearrange("p g u m -> p g m u"),
+            )
 
         def quantise_c(i):
-            t["c_codes", i] = work.tile([P, H_PASSES * P], U32, name="c_codes", bufs=3 + LAG, align_bytes=64)
-            t["c_scales", i] = work.tile([P, H_PASSES * P], U8, name="c_scales", bufs=3 + LAG, align_bytes=64)
+            tiles["c_codes", i] = work.tile([P, H_PASSES * P], U32, name="c_codes", bufs=3 + LAG, align_bytes=64)
+            tiles["c_scales", i] = work.tile([P, H_PASSES * P], U8, name="c_scales", bufs=3 + LAG, align_bytes=64)
             nc.vector.quantize_mx(
-                out=t["c_codes", i][:].bitcast(E5M2X4),
-                scales=t["c_scales", i][:],
-                in_=t["c_grouped", i][:].rearrange("p g m j -> p (g m j)"),
+                out=tiles["c_codes", i][:].bitcast(E5M2X4),
+                scales=tiles["c_scales", i][:],
+                in_=tiles["c_grouped", i][:, :H],
             )
 
-        def evaluate(i, b):
-            t["v_bank", i, b] = psum.tile([P, BANK], F32, name="bank", bufs=8)
-            for g in range(H_PASSES):
-                nc.tensor.matmul_mx(
-                    out=t["v_bank", i, b][:],
-                    lhsT=t["c_codes", i][:, g * P : (g + 1) * P].bitcast(E5M2X4),
-                    lhsT_scale=t["c_scales", i][:, g * P : (g + 1) * P],
-                    rhs=t["basis_codes", H_PASSES * b + g][:].bitcast(E4M3X4),
-                    rhs_scale=t["basis_scales", H_PASSES * b + g][:],
-                    start=(g == 0),
-                    stop=(g == H_PASSES - 1),
+        def evaluate(i, half):
+            for b in (2 * half, 2 * half + 1):
+                tiles["v_bank", i, b] = psum.tile([P, BANK], F32, name="bank")
+                for hg in range(H_PASSES):
+                    nc.tensor.matmul_mx(
+                        out=tiles["v_bank", i, b][:],
+                        lhsT=tiles["c_codes", i][:, hg * P : (hg + 1) * P].bitcast(E5M2X4),
+                        lhsT_scale=tiles["c_scales", i][:, hg * P : (hg + 1) * P],
+                        rhs=tiles["basis_codes", H_PASSES * b + hg][:].bitcast(E4M3X4),
+                        rhs_scale=tiles["basis_scales", H_PASSES * b + hg][:],
+                        start=(hg == 0),
+                        stop=(hg == H_PASSES - 1),
+                    )
+
+        def subtract(i, half):
+            tiles["r", i, half] = work.tile([P, HALF], F32, name="residual", bufs=7)
+            for side in range(2):
+                cols = slice(side * BANK, (side + 1) * BANK)
+                nc.vector.tensor_tensor(
+                    out=tiles["r", i, half][:, cols],
+                    in0=tiles["obs", i, half][:, cols],
+                    in1=tiles["v_bank", i, 2 * half + side][:],
+                    op=ALU.subtract,
                 )
 
-        def subtract(i, b):
-            half, side = divmod(b, 2)
-            if side == 0:
-                t["r", i, half] = work.tile([P, HALF], F32, name="residual", bufs=4)
-            nc.vector.tensor_tensor(
-                out=t["r", i, half][:, side * BANK : (side + 1) * BANK],
-                in0=t["obs", i][:, b * BANK : (b + 1) * BANK],
-                in1=t["v_bank", i, b][:],
-                op=ALU.subtract,
-            )
-
-        def pieces(i, half):
-            if i == M_TILES - 1 and half == 1:
-                return [slice(c, c + FINE) for c in range(0, HALF, FINE)]
+        def spans(i, half):
+            if (i, half) == (ROW_TILES - 1, 1):
+                return [slice(0, BANK), slice(BANK, HALF)]
             return [slice(0, HALF)]
 
         def square(i, half):
-            t["sq", i, half] = work.tile([P, HALF], F32, name="squares", bufs=3)
-            for c in pieces(i, half):
-                nc.scalar.activation(out=t["sq", i, half][:, c], in_=t["r", i, half][:, c], func=ACT.Square)
+            tiles["w", i, half] = work.tile([P, HALF], F32, name="weight", bufs=6)
+            for cols in spans(i, half):
+                nc.scalar.activation(out=tiles["w", i, half][:, cols], in_=tiles["r", i, half][:, cols], func=ACT.Square)
 
         def gauss(i, half):
-            t["w", i, half] = work.tile([P, HALF], F32, name="weights", bufs=3)
-            for c in pieces(i, half):
-                nc.scalar.activation(out=t["w", i, half][:, c], in_=t["sq", i, half][:, c], func=ACT.Exp, scale=-0.5)
+            for cols in spans(i, half):
+                w = tiles["w", i, half][:, cols]
+                nc.scalar.activation(out=w, in_=w, func=ACT.Exp, scale=-0.5)
 
-        def weigh(i, half):
-            res = work.tile([P, HALF], F32, name="result", bufs=4)
-            eng = nc.gpsimd if (GP and half == 1) else nc.vector
-            for c in pieces(i, half):
-                eng.tensor_tensor(out=res[:, c], in0=t["r", i, half][:, c], in1=t["w", i, half][:, c], op=ALU.mult)
-                nc.sync.dma_start(out=out[i * P : (i + 1) * P, half * HALF : (half + 1) * HALF][:, c], in_=res[:, c])
+        def weigh(i, half, engine, result=None):
+            if result is None:
+                result = tiles["w", i, half][:]
+            for cols in spans(i, half):
+                engine.tensor_tensor(
+                    out=result[:, cols], in0=tiles["r", i, half][:, cols], in1=tiles["w", i, half][:, cols], op=ALU.mult
+                )
+                nc.sync.dma_start(out=out[i * P : (i + 1) * P, half * HALF : (half + 1) * HALF][:, cols], in_=result[:, cols])
 
-        def when(i, f, *rest):
-            if 0 <= i < M_TILES:
-                f(i, *rest)
+        def on_tile(i, stage, *rest):
+            if 0 <= i < ROW_TILES:
+                stage(i, *rest)
+
+        def pieces_of(s):
+            first = 2 * (s + 2)
+            return (first, first + 1) if 0 <= first < PIECES else ()
 
         nc.vector.memset(fit_plane[:].bitcast(I32), 0)
         make_identity(nc, ident[:])
-        if WARM:
-            warm = keep.tile([P, 1], F32, name="warm")
-            nc.scalar.activation(out=warm[:], in_=ident[:, 0:1], func=ACT.Exp)
-        for item in LOADS:
-            dict(v=load_vel, f=load_fit, b=load_basis, o=load_obs, s=load_small)[item[0]](int(item[1]))
 
-        for s in range(-3, M_TILES + LAG + 1):
-            first, second = UNITS.get(s, ((), ()))
-            r = s - LAG
-            if s >= 0:
-                when(s + 4, load_vel)
-                when(s + 2, load_obs)
-            when(s, evaluate, 0)
-            when(s, evaluate, 1)
-            when(s + 2, quantise_vel)
-            when(s + 1, apply_damp, 0)
-            when(s + 1, apply_damp, 1)
-            when(s + 3, turn_vel)
-            when(s + 1, turn_c)
-            when(r - 1, square, 1)
-            when(s - 1, gauss, 0)
-            when(s, subtract, 0)
-            when(s, subtract, 1)
-            when(s + 3, group_vel, 0)
-            when(s + 1, group_c)
-            for u in first:
-                group_basis(u)
-            when(s - 1, weigh, 0)
-            when(r, evaluate, 2)
-            when(r, evaluate, 3)
+        for s in range(FIRST_STEP, ROW_TILES + LAG):
+            on_tile(s + 3, load_vel)
+            on_tile(s, load_obs, 0)
+            on_tile(s - LAG, load_obs, 1)
+            for piece in pieces_of(s):
+                load_basis(piece)
+                if piece == 0:
+                    load_damp_and_fit()
+
+        for s in range(FIRST_STEP, ROW_TILES + LAG + 2):
+            left, right = s, s - LAG
+            shared = SHARED_FROM <= s <= SHARED_TO
+            pieces = pieces_of(s)
+            on_tile(s + 3, turn_vel)
+            on_tile(s + 1, turn_c)
+            on_tile(s + 2, quantise_vel)
+            for piece in pieces_of(s - 1):
+                quantise_basis(piece)
+            on_tile(s, quantise_c)
+            if pieces and s < 0:
+                group_basis(pieces[0], nc.vector)
+            elif pieces:
+                group_basis(pieces[0], nc.gpsimd, tiles["c_grouped", s][:])
+            on_tile(right - 1, square, 1)
+            on_tile(left - 2, gauss, 0)
+            if shared and right >= 2:
+                weigh(right - 2, 1, nc.vector)
+                weigh(left - 3, 0, nc.gpsimd, tiles["r", right - 2, 1][:])
+            elif shared:
+                weigh(left - 3, 0, nc.gpsimd, tiles["c_grouped", s][:].bitcast(F32))
+            on_tile(left - 1, subtract, 0)
+            on_tile(s + 3, group_vel)
+            on_tile(s + 1, group_c)
             if s == -2:
                 spread_damp()
-            when(s + 2, project, 0)
-            when(s + 2, project, 1)
-            when(r - 1, gauss, 1)
-            when(s + 3, group_vel, 1)
-            when(s + 1, quantise_c)
-            when(r, subtract, 2)
-            when(r, subtract, 3)
-            when(s, square, 0)
-            for u in second:
-                group_basis(u)
-            when(r - 1, weigh, 1)
-            for u in first + second:
-                quantise_basis(u)
+            on_tile(s + 2, project)
+            on_tile(s + 2, apply_damp)
+            if pieces:
+                group_basis(pieces[1], nc.scalar)
+            on_tile(right - 1, gauss, 1)
+            on_tile(right, evaluate, 1)
+            on_tile(left, evaluate, 0)
+            on_tile(right, subtract, 1)
+            if not shared:
+                on_tile(left - 3, weigh, 0, nc.vector)
+                on_tile(right - 2, weigh, 1, nc.vector)
+            on_tile(left - 1, square, 0)

@@ -25,14 +25,17 @@ K_PASSES = K // PASS
 H_PASSES = H // PASS
 ROW_TILES = M // P
 HALF = N // 2
+LEFT, RIGHT = 0, 1
 PIECES = (N // BANK) * H_PASSES
 
 FIRST_STEP = -3
+FIT_STEP = FIRST_STEP + 1
 LAG = 2
-SHARED_FROM = 3
-SHARED_TO = 8
-VEL_SPLIT_FROM = 8
-ACTCOPY = 0
+CATCH_UP = 2
+SHARED_STEPS = range(2, ROW_TILES)
+VEL_SPLIT_FROM = 6
+RESIDUAL_BUFS = 8
+WEIGHT_BUFS = 6
 
 
 def tile_vad_harmonic_residuals_s9_kernel(tc, vel, fit_words, fit_scales, damp, basis, obs, out):
@@ -102,8 +105,6 @@ def tile_vad_harmonic_residuals_s9_kernel(tc, vel, fit_words, fit_scales, damp, 
             src = tiles["basis", piece][:].rearrange("p t (c i) -> p c t i", i=4)
             if engine is nc.vector:
                 nc.vector.tensor_copy(out=dst, in_=src)
-            elif ACTCOPY and piece == 1:
-                nc.scalar.activation(out=dst, in_=src, func=ACT.Copy)
             else:
                 nc.scalar.copy(out=dst, in_=src)
 
@@ -207,7 +208,7 @@ def tile_vad_harmonic_residuals_s9_kernel(tc, vel, fit_words, fit_scales, damp, 
                     )
 
         def subtract(i, half):
-            tiles["r", i, half] = work.tile([P, HALF], F32, name="residual", bufs=7)
+            tiles["r", i, half] = work.tile([P, HALF], F32, name="residual", bufs=RESIDUAL_BUFS)
             for side in range(2):
                 cols = slice(side * BANK, (side + 1) * BANK)
                 nc.vector.tensor_tensor(
@@ -218,12 +219,12 @@ def tile_vad_harmonic_residuals_s9_kernel(tc, vel, fit_words, fit_scales, damp, 
                 )
 
         def spans(i, half):
-            if (i, half) == (ROW_TILES - 1, 1):
+            if (i, half) == (ROW_TILES - 1, LEFT):
                 return [slice(0, BANK), slice(BANK, HALF)]
             return [slice(0, HALF)]
 
         def square(i, half):
-            tiles["w", i, half] = work.tile([P, HALF], F32, name="weight", bufs=6)
+            tiles["w", i, half] = work.tile([P, HALF], F32, name="weight", bufs=WEIGHT_BUFS)
             for cols in spans(i, half):
                 nc.scalar.activation(out=tiles["w", i, half][:, cols], in_=tiles["r", i, half][:, cols], func=ACT.Square)
 
@@ -246,27 +247,39 @@ def tile_vad_harmonic_residuals_s9_kernel(tc, vel, fit_words, fit_scales, damp, 
                 stage(i, *rest)
 
         def pieces_of(s):
-            first = 2 * (s + 2)
-            return (first, first + 1) if 0 <= first < PIECES else ()
+            first = H_PASSES * (s - FIT_STEP)
+            return list(range(first, first + H_PASSES)) if 0 <= first < PIECES else []
+
+        def rights_before(s):
+            return max(0, min(s, CATCH_UP * (s - LAG), ROW_TILES))
+
+        def rights_of(s):
+            return range(rights_before(s), rights_before(s + 1))
 
         nc.vector.memset(fit_plane[:].bitcast(I32), 0)
         make_identity(nc, ident[:])
 
-        for s in range(FIRST_STEP, ROW_TILES + LAG):
+        for s in range(FIRST_STEP, ROW_TILES):
             on_tile(s + 3, load_vel)
-            on_tile(s, load_obs, 0)
-            on_tile(s - LAG, load_obs, 1)
+            on_tile(s, load_obs, LEFT)
+            for i in rights_of(s):
+                load_obs(i, RIGHT)
             for piece in pieces_of(s):
                 load_basis(piece)
                 if piece == 0:
                     load_damp_and_fit()
 
-        for s in range(FIRST_STEP, ROW_TILES + LAG + 2):
-            left, right = s, s - LAG
-            shared = SHARED_FROM <= s <= SHARED_TO
+        weighted = []
+        for s in range(FIRST_STEP, ROW_TILES + 3):
             pieces = pieces_of(s)
+            left_at_once = range(LAG)
+            fresh = [(i, RIGHT) for i in rights_of(s - 1)]
+            if s - 1 in left_at_once:
+                fresh.append((s - 1, LEFT))
+
             on_tile(s + 3, turn_vel)
             on_tile(s + 1, turn_c)
+
             on_tile(s + 2, quantise_vel)
             for piece in pieces_of(s - 1):
                 quantise_basis(piece)
@@ -275,27 +288,44 @@ def tile_vad_harmonic_residuals_s9_kernel(tc, vel, fit_words, fit_scales, damp, 
                 group_basis(pieces[0], nc.vector)
             elif pieces:
                 group_basis(pieces[0], nc.gpsimd, tiles["c_grouped", s][:])
-            on_tile(right - 1, square, 1)
-            on_tile(left - 2, gauss, 0)
-            if shared and right >= 2:
-                weigh(right - 2, 1, nc.vector)
-                weigh(left - 3, 0, nc.gpsimd, tiles["r", right - 2, 1][:])
-            elif shared:
-                weigh(left - 3, 0, nc.gpsimd, tiles["c_grouped", s][:].bitcast(F32))
-            on_tile(left - 1, subtract, 0)
+            if s in SHARED_STEPS and len(weighted) >= 2:
+                weigh(*weighted[0], nc.vector)
+                weigh(*weighted[1], nc.gpsimd, tiles[("r",) + weighted[0]][:])
+                weighted = weighted[2:]
+            elif s in SHARED_STEPS:
+                weigh(*weighted[0], nc.gpsimd, tiles["c_grouped", s][:].bitcast(F32))
+                weighted = []
+
+            for key in fresh[:1]:
+                square(*key)
+            if s - 2 not in left_at_once:
+                on_tile(s - 2, gauss, LEFT)
+            for key in fresh[1:]:
+                square(*key)
+            if s - 1 not in left_at_once:
+                on_tile(s - 1, subtract, LEFT)
             on_tile(s + 3, group_vel)
             on_tile(s + 1, group_c)
-            if s == -2:
+            if s == FIT_STEP:
                 spread_damp()
             on_tile(s + 2, project)
             on_tile(s + 2, apply_damp)
+            for key in fresh:
+                gauss(*key)
             if pieces:
                 group_basis(pieces[1], nc.scalar)
-            on_tile(right - 1, gauss, 1)
-            on_tile(right, evaluate, 1)
-            on_tile(left, evaluate, 0)
-            on_tile(right, subtract, 1)
-            if not shared:
-                on_tile(left - 3, weigh, 0, nc.vector)
-                on_tile(right - 2, weigh, 1, nc.vector)
-            on_tile(left - 1, square, 0)
+
+            for i in rights_of(s):
+                evaluate(i, RIGHT)
+            on_tile(s, evaluate, LEFT)
+            for i in rights_of(s):
+                subtract(i, RIGHT)
+            if s in left_at_once:
+                subtract(s, LEFT)
+            for key in weighted:
+                weigh(*key, nc.vector)
+            if s - 1 not in left_at_once:
+                on_tile(s - 1, square, LEFT)
+
+            weighted = [(s - 2, LEFT)] if LAG <= s - 2 < ROW_TILES else []
+            weighted = weighted + fresh

@@ -66,13 +66,15 @@ def tile_vad_harmonic_residuals_s9_kernel(tc, vel, fit_words, fit_scales, damp, 
             rows = basis[g * PASS : (g + 1) * PASS, b * BANK : (b + 1) * BANK]
             nc.sync.dma_start(out=tiles["basis", piece][:], in_=rows.rearrange("(p t) n -> p t n", t=PACK))
 
-        def load_damp_and_fit():
+        def load_damp_and_scales():
             nc.sync.dma_start(out=damp_rows[:], in_=damp.rearrange("(g p t) -> p g t", g=H_PASSES, t=PACK))
-            for q in range(4):
+            for r in range(4):
                 nc.sync.dma_start(
-                    out=fit_plane[32 * q : 32 * q + 4].bitcast(I32),
-                    in_=fit_scales[:, 4 * q : 4 * q + 4, :].bitcast(I32).rearrange("g r c -> r g c"),
+                    out=fit_plane[r:P:32].bitcast(I32),
+                    in_=fit_scales[:, r:16:4, :].bitcast(I32).rearrange("g q c -> q g c"),
                 )
+
+        def load_fit():
             for j in range(K_PASSES // 2):
                 tiles["fit", j] = keep.tile([P, 2, 2 * H], U8, name="fit%d" % j, align_bytes=64)
                 nc.sync.dma_start(
@@ -261,13 +263,15 @@ def tile_vad_harmonic_residuals_s9_kernel(tc, vel, fit_words, fit_scales, damp, 
 
         for s in range(FIRST_STEP, ROW_TILES):
             on_tile(s + 3, load_vel)
+            if s == FIRST_STEP:
+                load_damp_and_scales()
             on_tile(s, load_obs, LEFT)
             for i in rights_of(s):
                 load_obs(i, RIGHT)
             for piece in pieces_of(s):
                 load_basis(piece)
                 if piece == 0:
-                    load_damp_and_fit()
+                    load_fit()
 
         weighted = []
         for s in range(FIRST_STEP, ROW_TILES + 3):

from contextlib import ExitStack

import concourse.mybir as mybir
from concourse.masks import make_identity

M, K, H, N = 1024, 2048, 1024, 2048
FLOPS = 2 * M * K * H + 2 * M * H * N

F32 = mybir.dt.float32
BF16 = mybir.dt.bfloat16
U32 = mybir.dt.uint32
I32 = mybir.dt.int32
U8 = mybir.dt.uint8
E4M3X4 = mybir.dt.float8_e4m3fn_x4
E5M2X4 = mybir.dt.float8_e5m2_x4
E2M1X4 = mybir.dt.float4_e2m1fn_x4
ALU = mybir.AluOpType
ACT = mybir.ActivationFunctionType

P = 128
PACK = 4
PASS = P * PACK
BANK = 512
K_PASSES = K // PASS
H_PASSES = H // PASS
ROW_TILES = M // P
HALF = N // 2
LEFT, RIGHT = 0, 1
PIECES = (N // BANK) * H_PASSES

FIRST_STEP = -3
FIT_STEP = FIRST_STEP + 1
LAG = 2
CATCH_UP = 2
SHARED_STEPS = range(2, ROW_TILES)
VEL_SPLIT_FROM = 6
RESIDUAL_BUFS = 8
WEIGHT_BUFS = 6


def tile_vad_harmonic_residuals_s9_kernel(tc, vel, fit_words, fit_scales, damp, basis, obs, out):
    nc = tc.nc
    with ExitStack() as ctx:
        keep = ctx.enter_context(tc.tile_pool(name="keep", bufs=1))
        work = ctx.enter_context(tc.tile_pool(name="work", bufs=2))
        psum = ctx.enter_context(tc.psum_pool(name="psum", bufs=8))
        ctx.enter_context(tc.manual_schedule())

        ident = keep.tile([P, P], F32, name="ident")
        fit_plane = keep.tile([P, K_PASSES, H], U8, name="fit_plane", align_bytes=64)
        damp_rows = keep.tile([P, H_PASSES, PACK], BF16, name="damp_rows")
        damp_all = keep.tile([P, H], BF16, name="damp_all")
        tiles = {}

        def load_vel(i):
            tiles["vel", i] = keep.tile([P, K], BF16, name="vel%d" % i)
            nc.sync.dma_start(out=tiles["vel", i][:], in_=vel[i * P : (i + 1) * P, :])

        def load_obs(i, half):
            tiles["obs", i, half] = keep.tile([P, HALF], BF16, name="obs%d_%d" % (i, half))
            nc.sync.dma_start(out=tiles["obs", i, half][:], in_=obs[i * P : (i + 1) * P, half * HALF : (half + 1) * HALF])

        def load_basis(piece):
            b, g = divmod(piece, H_PASSES)
            tiles["basis", piece] = keep.tile([P, PACK, BANK], BF16, name="basis%d" % piece)
            rows = basis[g * PASS : (g + 1) * PASS, b * BANK : (b + 1) * BANK]
            nc.sync.dma_start(out=tiles["basis", piece][:], in_=rows.rearrange("(p t) n -> p t n", t=PACK))

        def load_damp_and_scales():
            nc.sync.dma_start(out=damp_rows[:], in_=damp.rearrange("(g p t) -> p g t", g=H_PASSES, t=PACK))
            for r in range(4):
                nc.sync.dma_start(
                    out=fit_plane[r:P:32].bitcast(I32),
                    in_=fit_scales[:, r:16:4, :].bitcast(I32).rearrange("g q c -> q g c"),
                )

        def load_fit():
            for j in range(K_PASSES // 2):
                tiles["fit", j] = keep.tile([P, 2, 2 * H], U8, name="fit%d" % j, align_bytes=64)
                nc.sync.dma_start(
                    out=tiles["fit", j][:].bitcast(I32),
                    in_=fit_words[2 * j : 2 * j + 2].bitcast(I32).rearrange("g p c -> p g c"),
                )

        def spread_damp():
            bank = psum.tile([P, H_PASSES * 2, P], F32, name="bank")
            words = damp_rows[:].rearrange("p g t -> p (g t)").bitcast(F32)
            for c in range(H_PASSES * 2):
                nc.tensor.transpose(bank[:, c, :], words[:, c : c + 1].to_broadcast([P, P]), ident[:])
            nc.scalar.copy(out=damp_all[:].bitcast(F32), in_=bank[:].rearrange("m c p -> m (c p)"))

        def group_basis(piece, engine, grouped=None):
            if grouped is None:
                grouped = work.tile([P, BANK * PACK], BF16, name="basis_grouped", align_bytes=64)[:]
            tiles["basis_grouped", piece] = grouped
            if engine is nc.gpsimd:
                nc.gpsimd.tensor_scalar(
                    out=grouped.rearrange("p (n t) -> p n t", t=PACK),
                    in0=tiles["basis", piece][:].rearrange("p t n -> p n t"),
                    scalar1=1.0,
                    scalar2=0.0,
                    op0=ALU.mult,
                    op1=ALU.add,
                )
                return
            dst = grouped.rearrange("p (c i t) -> p c t i", i=4, t=PACK)
            src = tiles["basis", piece][:].rearrange("p t (c i) -> p c t i", i=4)
            if engine is nc.vector:
                nc.vector.tensor_copy(out=dst, in_=src)
            else:
                nc.scalar.copy(out=dst, in_=src)

        def quantise_basis(piece):
            tiles["basis_codes", piece] = keep.tile([P, BANK], U32, name="basis_codes%d" % piece, align_bytes=64)
            tiles["basis_scales", piece] = keep.tile([P, BANK], U8, name="basis_scales%d" % piece, align_bytes=64)
            nc.vector.quantize_mx(
                out=tiles["basis_codes", piece][:].bitcast(E4M3X4),
                scales=tiles["basis_scales", piece][:],
                in_=tiles["basis_grouped", piece],
            )

        def turn_vel(i):
            words = tiles["vel", i][:].bitcast(F32)
            for j in range(K_PASSES // 2):
                tiles["vel_bank", i, j] = psum.tile([P, 2, 2, P], F32, name="bank")
                for g in range(2):
                    w0 = (2 * j + g) * PASS // 2
                    for u in range(2):
                        nc.tensor.transpose(tiles["vel_bank", i, j][:, g, u, :], words[:, w0 + u : w0 + PASS // 2 : 2], ident[:])

        def group_vel(i):
            tiles["vel_grouped", i] = work.tile([P, K_PASSES, P, PACK], BF16, name="vel_grouped", align_bytes=64)
            for j in range(K_PASSES // 2):
                copy = nc.vector.tensor_copy if (i >= VEL_SPLIT_FROM and j == 1) else nc.scalar.copy
                copy(
                    out=tiles["vel_grouped", i][:, 2 * j : 2 * j + 2].bitcast(F32),
                    in_=tiles["vel_bank", i, j][:].rearrange("p g u m -> p g m u"),
                )

        def quantise_vel(i):
            tiles["vel_codes", i] = work.tile([P, K_PASSES * P], U32, name="vel_codes", align_bytes=64)
            tiles["vel_scales", i] = work.tile([P, K_PASSES * P], U8, name="vel_scales", align_bytes=64)
            nc.vector.quantize_mx(
                out=tiles["vel_codes", i][:].bitcast(E4M3X4),
                scales=tiles["vel_scales", i][:],
                in_=tiles["vel_grouped", i][:].rearrange("p g m t -> p (g m t)"),
            )

        def project(i):
            for hg in range(H_PASSES):
                tiles["c_bank", i, hg] = psum.tile([P, BANK], F32, name="bank")
                for g in range(K_PASSES):
                    nc.tensor.matmul_mx(
                        out=tiles["c_bank", i, hg][:],
                        lhsT=tiles["vel_codes", i][:, g * P : (g + 1) * P].bitcast(E4M3X4),
                        lhsT_scale=tiles["vel_scales", i][:, g * P : (g + 1) * P],
                        rhs=tiles["fit", g // 2][:, g % 2, 2 * hg * BANK : 2 * (hg + 1) * BANK].bitcast(E2M1X4),
                        rhs_scale=fit_plane[:, g, hg * BANK : (hg + 1) * BANK],
                        start=(g == 0),
                        stop=(g == K_PASSES - 1),
                    )

        def apply_damp(i):
            tiles["c_rows", i] = work.tile([P, H], BF16, name="c_rows")
            for hg in range(H_PASSES):
                cols = slice(hg * BANK, (hg + 1) * BANK)
                nc.vector.tensor_tensor(
                    out=tiles["c_rows", i][:, cols].rearrange("m (u p e) -> m u p e", u=2, e=2),
                    in0=tiles["c_bank", i, hg][:].rearrange("m (p u e) -> m u p e", u=2, e=2),
                    in1=damp_all[:, cols].rearrange("m (u p e) -> m u p e", u=2, e=2),
                    op=ALU.mult,
                )

        def turn_c(i):
            words = tiles["c_rows", i][:].bitcast(F32)
            tiles["c_turned", i] = psum.tile([P, H_PASSES, 2, P], F32, name="bank")
            for hg in range(H_PASSES):
                for u in range(2):
                    w0 = (2 * hg + u) * P
                    nc.tensor.transpose(tiles["c_turned", i][:, hg, u, :], words[:, w0 : w0 + P], ident[:])

        def group_c(i):
            tiles["c_grouped", i] = work.tile([P, 2 * H], BF16, name="c_grouped", bufs=3, align_bytes=64)
            nc.scalar.copy(
                out=tiles["c_grouped", i][:, :H].bitcast(F32).rearrange("p (g m u) -> p g m u", g=H_PASSES, u=2),
                in_=tiles["c_turned", i][:].rearrange("p g u m -> p g m u"),
            )

        def quantise_c(i):
            tiles["c_codes", i] = work.tile([P, H_PASSES * P], U32, name="c_codes", bufs=3 + LAG, align_bytes=64)
            tiles["c_scales", i] = work.tile([P, H_PASSES * P], U8, name="c_scales", bufs=3 + LAG, align_bytes=64)
            nc.vector.quantize_mx(
                out=tiles["c_codes", i][:].bitcast(E5M2X4),
                scales=tiles["c_scales", i][:],
                in_=tiles["c_grouped", i][:, :H],
            )

        def evaluate(i, half):
            for b in (2 * half, 2 * half + 1):
                tiles["v_bank", i, b] = psum.tile([P, BANK], F32, name="bank")
                for hg in range(H_PASSES):
                    nc.tensor.matmul_mx(
                        out=tiles["v_bank", i, b][:],
                        lhsT=tiles["c_codes", i][:, hg * P : (hg + 1) * P].bitcast(E5M2X4),
                        lhsT_scale=tiles["c_scales", i][:, hg * P : (hg + 1) * P],
                        rhs=tiles["basis_codes", H_PASSES * b + hg][:].bitcast(E4M3X4),
                        rhs_scale=tiles["basis_scales", H_PASSES * b + hg][:],
                        start=(hg == 0),
                        stop=(hg == H_PASSES - 1),
                    )

        def subtract(i, half):
            tiles["r", i, half] = work.tile([P, HALF], F32, name="residual", bufs=RESIDUAL_BUFS)
            for side in range(2):
                cols = slice(side * BANK, (side + 1) * BANK)
                nc.vector.tensor_tensor(
                    out=tiles["r", i, half][:, cols],
                    in0=tiles["obs", i, half][:, cols],
                    in1=tiles["v_bank", i, 2 * half + side][:],
                    op=ALU.subtract,
                )

        def spans(i, half):
            if (i, half) == (ROW_TILES - 1, LEFT):
                return [slice(0, BANK), slice(BANK, HALF)]
            return [slice(0, HALF)]

        def square(i, half):
            tiles["w", i, half] = work.tile([P, HALF], F32, name="weight", bufs=WEIGHT_BUFS)
            for cols in spans(i, half):
                nc.scalar.activation(out=tiles["w", i, half][:, cols], in_=tiles["r", i, half][:, cols], func=ACT.Square)

        def gauss(i, half):
            for cols in spans(i, half):
                w = tiles["w", i, half][:, cols]
                nc.scalar.activation(out=w, in_=w, func=ACT.Exp, scale=-0.5)

        def weigh(i, half, engine, result=None):
            if result is None:
                result = tiles["w", i, half][:]
            for cols in spans(i, half):
                engine.tensor_tensor(
                    out=result[:, cols], in0=tiles["r", i, half][:, cols], in1=tiles["w", i, half][:, cols], op=ALU.mult
                )
                nc.sync.dma_start(out=out[i * P : (i + 1) * P, half * HALF : (half + 1) * HALF][:, cols], in_=result[:, cols])

        def on_tile(i, stage, *rest):
            if 0 <= i < ROW_TILES:
                stage(i, *rest)

        def pieces_of(s):
            first = H_PASSES * (s - FIT_STEP)
            return list(range(first, first + H_PASSES)) if 0 <= first < PIECES else []

        def rights_before(s):
            return max(0, min(s, CATCH_UP * (s - LAG), ROW_TILES))

        def rights_of(s):
            return range(rights_before(s), rights_before(s + 1))

        nc.vector.memset(fit_plane[:].bitcast(I32), 0)
        make_identity(nc, ident[:])

        for s in range(FIRST_STEP, ROW_TILES):
            on_tile(s + 3, load_vel)
            if s == FIRST_STEP:
                load_damp_and_scales()
            on_tile(s, load_obs, LEFT)
            for i in rights_of(s):
                load_obs(i, RIGHT)
            for piece in pieces_of(s):
                load_basis(piece)
                if piece == 0:
                    load_fit()

        weighted = []
        for s in range(FIRST_STEP, ROW_TILES + 3):
            pieces = pieces_of(s)
            left_at_once = range(LAG)
            fresh = [(i, RIGHT) for i in rights_of(s - 1)]
            if s - 1 in left_at_once:
                fresh.append((s - 1, LEFT))

            on_tile(s + 3, turn_vel)
            on_tile(s + 1, turn_c)

            on_tile(s + 2, quantise_vel)
            for piece in pieces_of(s - 1):
                quantise_basis(piece)
            on_tile(s, quantise_c)
            if pieces and s < 0:
                group_basis(pieces[0], nc.vector)
            elif pieces:
                group_basis(pieces[0], nc.gpsimd, tiles["c_grouped", s][:])
            if s in SHARED_STEPS and len(weighted) >= 2:
                weigh(*weighted[0], nc.vector)
                weigh(*weighted[1], nc.gpsimd, tiles[("r",) + weighted[0]][:])
                weighted = weighted[2:]
            elif s in SHARED_STEPS:
                weigh(*weighted[0], nc.gpsimd, tiles["c_grouped", s][:].bitcast(F32))
                weighted = []

            for key in fresh[:1]:
                square(*key)
            if s - 2 not in left_at_once:
                on_tile(s - 2, gauss, LEFT)
            for key in fresh[1:]:
                square(*key)
            if s - 1 not in left_at_once:
                on_tile(s - 1, subtract, LEFT)
            on_tile(s + 3, group_vel)
            on_tile(s + 1, group_c)
            if s == FIT_STEP:
                spread_damp()
            on_tile(s + 2, project)
            on_tile(s + 2, apply_damp)
            for key in fresh:
                gauss(*key)
            if pieces:
                group_basis(pieces[1], nc.scalar)

            for i in rights_of(s):
                evaluate(i, RIGHT)
            on_tile(s, evaluate, LEFT)
            for i in rights_of(s):
                subtract(i, RIGHT)
            if s in left_at_once:
                subtract(s, LEFT)
            for key in weighted:
                weigh(*key, nc.vector)
            if s - 1 not in left_at_once:
                on_tile(s - 1, square, LEFT)

            weighted = [(s - 2, LEFT)] if LAG <= s - 2 < ROW_TILES else []
            weighted = weighted + fresh
